import numpy as np
import ml_dtypes


def mxq(x, axis, fmt="e4m3"):
    dtype, down = {"e4m3": (ml_dtypes.float8_e4m3fn, 7), "e5m2": (ml_dtypes.float8_e5m2, 14)}[fmt]
    v = np.moveaxis(np.asarray(x, np.float32).astype(ml_dtypes.bfloat16).astype(np.float64), axis, -1)
    blocks = v.reshape(v.shape[:-1] + (-1, 32))
    amax = np.abs(blocks).max(-1, keepdims=True)
    byte = np.maximum(np.where(amax > 0, np.frexp(amax)[1] - 1 + 127, 0) - down, 1)
    scale = np.exp2(byte - 127.0)
    codes = (blocks / scale).astype(np.float32).astype(dtype).astype(np.float64)
    return np.moveaxis((codes * scale).reshape(v.shape), -1, axis)


WIDE = False


def mx_kscale(k):
    if not WIDE:
        return np.ones(k)
    levels = np.array([10, -10, 5, -5, 0])
    if k % 512:
        return np.exp2(np.random.permutation(np.resize(levels, k // 32))).repeat(32)
    a = np.empty((k // 512, 16))
    for p in range(k // 512):
        a[p, :8] = np.random.permutation(np.resize(levels, 8))
        for g in range(8):
            far = levels[np.abs(levels - a[p, g]) >= 10]
            a[p, g + 8] = far[np.random.randint(len(far))]
    return np.exp2(a.ravel()).repeat(32)


BF16 = ml_dtypes.bfloat16


def bf(x):
    return np.asarray(x, np.float32).astype(BF16)


def f64(x):
    return np.asarray(x).astype(np.float64)


E2M1 = np.array([0.0, 0.5, 1.0, 1.5, 2.0, 3.0, 4.0, 6.0, -0.0, -0.5, -1.0, -1.5, -2.0, -3.0, -4.0, -6.0])


def pack_weight(w, fmt):
    k, n = w.shape
    w = f64(bf(w)).reshape(k // 32, 32, n)
    amax = np.abs(w).max(1)
    if fmt == "e4m3":
        byte = np.frexp(amax)[1] - 1 + 127 - 7
    else:
        mant, ex = np.frexp(amax / 6.0)
        byte = np.where(mant > 0.5, ex, ex - 1) + 127
    byte = np.clip(np.where(amax > 0, byte, 1), 1, 254)
    scaled = (w * np.exp2(127.0 - byte)[:, None, :]).reshape(k, n).astype(np.float32)
    by_word = np.ascontiguousarray(scaled.reshape(k // 512, 128, 4, n).transpose(0, 1, 3, 2))
    if fmt == "e4m3":
        words = by_word.astype(ml_dtypes.float8_e4m3fn).view(np.uint8)
    else:
        c = by_word.astype(ml_dtypes.float4_e2m1fn).view(np.uint8) & 0xF
        words = c[..., 0::2] | (c[..., 1::2] << 4)
    return np.ascontiguousarray(words), np.ascontiguousarray(byte.astype(np.uint8).reshape(k // 512, 16, n))


def unpack_weight(words, scales, fmt):
    g, p, n, _ = words.shape
    if fmt == "e4m3":
        vals = np.ascontiguousarray(words).view(ml_dtypes.float8_e4m3fn).astype(np.float64)
    else:
        nib = np.empty((g, p, n, 4), np.uint8)
        nib[..., 0::2] = words & 0xF
        nib[..., 1::2] = words >> 4
        vals = E2M1[nib]
    vals = vals * np.repeat(np.exp2(scales.astype(np.float64) - 127.0), 8, axis=1)[..., None]
    return vals.transpose(0, 1, 3, 2).reshape(g * 512, n)
def pack4(w):
    words, scales = pack_weight(w, "e2m1")
    return words.reshape(words.shape[0], 128, -1), scales


def unpack4(words, scales):
    return unpack_weight(words.reshape(words.shape[0], 128, -1, 2), scales, "e2m1")


Q, P, H, A, B = 1024, 1536, 1536, 1024, 512


def setup_inputs():
    s, u, t = mx_kscale(Q), mx_kscale(P), mx_kscale(H)
    c = H ** -0.25
    mode_words, mode_scales = pack4(np.random.standard_normal((Q, H)) * c * s[:, None] * t)
    test_words, test_scales = pack4(np.random.standard_normal((Q, A)) / np.sqrt(Q) / s[:, None])
    return {"mode_words": mode_words, "mode_scales": mode_scales,
            "test_words": test_words, "test_scales": test_scales,
            "fine_modes": bf(np.random.standard_normal((H, P)) * c * u / t[:, None]),
            "trial": bf(np.random.standard_normal((P, B)) / np.sqrt(P) / u[:, None]),
            "y_mode": bf(np.random.uniform(0.3, 1.7, H)),
            "y_ext": bf(0.5 * np.random.standard_normal((A, B)))}


def reference(mode_words, mode_scales, test_words, test_scales, fine_modes, trial, y_mode, y_ext):
    C = unpack4(mode_words, mode_scales)
    D = unpack4(test_words, test_scales)
    X = C.T @ D
    Z = mxq(f64(fine_modes), 1, "e4m3") @ mxq(f64(trial), 0, "e4m3")
    V = X * f64(y_mode)[:, None]
    Y = mxq(V, 0, "e4m3").T @ mxq(Z, 0, "e4m3")
    return Y + f64(y_ext)

@@ -1,0 +1,334 @@
+from contextlib import ExitStack
+
+import concourse.mybir as mybir
+from concourse.masks import make_identity
+
+Q, P, H, A, B = 1024, 1536, 1536, 1024, 512
+FLOPS = 2 * (Q * H * A + H * P * B + H * A * B)
+
+F32 = mybir.dt.float32
+BF16 = mybir.dt.bfloat16
+I32 = mybir.dt.int32
+U32 = mybir.dt.uint32
+U8 = mybir.dt.uint8
+FP8X4 = mybir.dt.float8_e4m3fn_x4
+FP4X4 = mybir.dt.float4_e2m1fn_x4
+COPY = mybir.ActivationFunctionType.Copy
+ADD = mybir.AluOpType.add
+
+PART = 128
+SLOTS = 4
+K_PASS = PART * SLOTS
+BANK = 512
+BANKS = 8
+Q_PASSES = Q // K_PASS
+P_PASSES = P // K_PASS
+H_PASSES = H // K_PASS
+A_HALVES = A // BANK
+A_TILES = A // PART
+B_TILES = B // PART
+ROW_PAIRS = 2
+
+
+def tile_aperture_mode_admittance_s12_kernel(
+    tc, mode_words, mode_scales, test_words, test_scales, fine_modes, trial, y_mode, y_ext, out
+):
+    nc = tc.nc
+    with ExitStack() as ctx:
+        keep = ctx.enter_context(tc.tile_pool(name="keep", bufs=1))
+        ring = ctx.enter_context(tc.tile_pool(name="ring", bufs=2))
+        psum = ctx.enter_context(tc.psum_pool(name="psum", bufs=1))
+        ctx.enter_context(tc.manual_schedule())
+
+        def kept(name, shape, dtype):
+            return keep.tile(shape, dtype, name=name, align_bytes=64)
+
+        def staged(name, shape, dtype, bufs):
+            return ring.tile(shape, dtype, name=name, tag=name, bufs=bufs, align_bytes=64)
+
+        taken = []
+
+        def next_bank(shape):
+            name = "bank%d" % (len(taken) % BANKS)
+            taken.append(name)
+            return psum.tile(shape, F32, name=name, tag=name)
+
+        def quantize(name, grouped, bufs):
+            if bufs:
+                codes = staged(name + "_codes", [PART, K_PASS], U32, bufs)
+                scales = staged(name + "_scales", [PART, K_PASS], U8, bufs)
+            else:
+                codes = kept(name + "_codes", [PART, K_PASS], U32)
+                scales = kept(name + "_scales", [PART, K_PASS], U8)
+            nc.vector.quantize_mx(out=codes[:].bitcast(FP8X4), scales=scales[:], in_=grouped[:])
+            return codes, scales
+
+        def interleave(name, rows):
+            grouped = staged(name, [PART, SLOTS * BANK], BF16, 2)
+            nc.vector.tensor_copy(
+                out=grouped[:].rearrange("p (n i t) -> p n t i", i=4, t=SLOTS),
+                in_=rows[:].rearrange("p t (n i) -> p n t i", i=4),
+            )
+            return grouped
+
+        c_words_hbm = mode_words.bitcast(I32).rearrange("c p w -> p c w")
+        d_words_hbm = test_words.bitcast(I32).rearrange("c p w -> p c w")
+        words_512 = K_PASS * 2 // 4
+
+        c_first = kept("c_first", [PART, Q_PASSES, 2 * K_PASS], U8)
+        c_rest = kept("c_rest", [PART, Q_PASSES, 2 * (H - K_PASS)], U8)
+        d_codes = [kept("d_codes%d" % half, [PART, Q_PASSES, 2 * BANK], U8) for half in range(A_HALVES)]
+        c_scales_raw = kept("c_scales_raw", [PART, Q_PASSES, H], U8)
+        d_scales = kept("d_scales", [PART, Q_PASSES, A], U8)
+        y_rows = kept("y_rows", [H_PASSES, K_PASS], BF16)
+        y_sorted = kept("y_sorted", [PART, K_PASS], F32)
+        y_cols = kept("y_cols", [PART, SLOTS, H_PASSES], F32)
+        ident = kept("ident", [PART, PART], F32)
+
+        nc.sync.dma_start(out=c_first[:].bitcast(I32), in_=c_words_hbm[:, :, :words_512])
+        nc.sync.dma_start(out=d_codes[0][:].bitcast(I32), in_=d_words_hbm[:, :, :words_512])
+        nc.scalar.dma_start(out=y_rows[:], in_=y_mode.rearrange("(g k) -> g k", g=H_PASSES))
+        nc.vector.memset(c_scales_raw[:].bitcast(I32), 0)
+        nc.vector.memset(d_scales[:].bitcast(I32), 0)
+        nc.vector.memset(y_sorted[:], 0.0)
+        make_identity(nc, ident[:])
+        c_scales_hbm = mode_scales.bitcast(I32).rearrange("c (quad r) w -> r quad c w", r=4)
+        d_scales_hbm = test_scales.bitcast(I32).rearrange("c (quad r) w -> r quad c w", r=4)
+        for r in range(4):
+            nc.sync.dma_start(out=c_scales_raw[r:PART:32].bitcast(I32), in_=c_scales_hbm[r])
+        for r in range(4):
+            nc.scalar.dma_start(out=d_scales[r:PART:32].bitcast(I32), in_=d_scales_hbm[r])
+
+        trial_rows = [kept("trial_rows%d" % c, [PART, SLOTS, B], BF16) for c in range(P_PASSES)]
+        fine_rows = {}
+        for g in range(H_PASSES):
+            for pair in range(ROW_PAIRS):
+                fine_rows[g, pair] = kept("fine_rows%d%d" % (g, pair), [PART, 2, P], BF16)
+        y_ext_sb = kept("y_ext_sb", [PART, A_TILES, B], BF16)
+
+        def load_trial(c):
+            rows = trial[c * K_PASS : (c + 1) * K_PASS, :]
+            nc.sync.dma_start(out=trial_rows[c][:], in_=rows.rearrange("(p t) n -> p t n", t=SLOTS))
+
+        def load_fine(g, pair):
+            first = g * K_PASS + pair * 2 * PART
+            rows = fine_modes[first : first + 2 * PART, :]
+            nc.sync.dma_start(out=fine_rows[g, pair][:], in_=rows.rearrange("(j p) k -> p j k", p=PART))
+
+        load_trial(0)
+        nc.sync.dma_start(out=d_codes[1][:].bitcast(I32), in_=d_words_hbm[:, :, words_512:])
+        nc.sync.dma_start(out=c_rest[:].bitcast(I32), in_=c_words_hbm[:, :, words_512:])
+        load_trial(1)
+        load_fine(0, 0)
+        load_trial(2)
+        load_fine(0, 1)
+        for g in range(1, H_PASSES):
+            for pair in range(ROW_PAIRS):
+                load_fine(g, pair)
+        nc.sync.dma_start(out=y_ext_sb[:], in_=y_ext.rearrange("(a p) n -> p a n", p=PART))
+
+        c_codes, c_scales = {}, {}
+
+        def sort_modes(g):
+            if g == 0:
+                words = c_first[:].bitcast(I32)
+            else:
+                words = c_rest[:].bitcast(I32)[:, :, (g - 1) * words_512 : g * words_512]
+            c_codes[g] = kept("c_codes%d" % g, [PART, Q_PASSES, SLOTS, 2 * PART], U8)
+            c_scales[g] = kept("c_scales%d" % g, [PART, Q_PASSES, SLOTS, PART], U8)
+            nc.vector.tensor_copy(
+                out=c_codes[g][:].bitcast(I32).rearrange("p c t (q w) -> p c t q w", w=4),
+                in_=words.rearrange("p c (q t w) -> p c t q w", t=SLOTS, w=4),
+            )
+            scale_words = c_scales_raw[:].bitcast(I32)[:, :, g * PART : (g + 1) * PART]
+            nc.vector.tensor_copy(
+                out=c_scales[g][:].bitcast(I32).rearrange("p c t (q w) -> p c t q w", w=2),
+                in_=scale_words.rearrange("p c (q t w) -> p c t q w", t=SLOTS, w=2),
+            )
+
+        def spread_y_mode():
+            nc.scalar.copy(
+                out=y_sorted[:H_PASSES].rearrange("g (t q r) -> g t q r", t=SLOTS, r=8),
+                in_=y_rows[:].rearrange("g (q t r) -> g t q r", t=SLOTS, r=8),
+            )
+            bank = next_bank([PART, SLOTS, PART])
+            for t in range(SLOTS):
+                nc.tensor.transpose(bank[:, t, :], y_sorted[:, t * PART : (t + 1) * PART], ident[:])
+            nc.scalar.copy(out=y_cols[:], in_=bank[:, :, :H_PASSES])
+
+        v_rows, v_grouped, v_mx = {}, {}, {}
+
+        def overlap_test(g, half):
+            v_rows[g, half] = staged("v_rows", [PART, SLOTS, BANK], BF16, 4)
+            for t in range(SLOTS):
+                bank = next_bank([PART, BANK])
+                for c in range(Q_PASSES):
+                    nc.tensor.matmul_mx(
+                        out=bank[:],
+                        lhsT=c_codes[g][:, c, t, :].bitcast(FP4X4),
+                        lhsT_scale=c_scales[g][:, c, t, :],
+                        rhs=d_codes[half][:, c, :].bitcast(FP4X4),
+                        rhs_scale=d_scales[:, c, half * BANK : (half + 1) * BANK],
+                        start=(c == 0),
+                        stop=(c == Q_PASSES - 1),
+                    )
+                nc.scalar.activation(out=v_rows[g, half][:, t, :], in_=bank[:], func=COPY, scale=y_cols[:, t, g : g + 1])
+
+        def group_v(g, half):
+            v_grouped[g, half] = interleave("v_grouped", v_rows[g, half])
+
+        def quantize_v(g, half):
+            v_mx[g, half] = quantize("v%d%d" % (g, half), v_grouped[g, half], 0)
+
+        trial_grouped, trial_mx = {}, {}
+
+        def group_trial(c):
+            trial_grouped[c] = interleave("trial_grouped", trial_rows[c])
+
+        def quantize_trial(c):
+            trial_mx[c] = quantize("trial%d" % c, trial_grouped[c], 0)
+
+        fine_sorted, fine_grouped, fine_mx = {}, {}, {}
+
+        def sort_fine(g, pair):
+            fine_sorted[g, pair] = staged("fine_sorted", [PART, 2 * P_PASSES, 2, PART], F32, 3)
+            words = fine_rows[g, pair][:].rearrange("p j k -> p (j k)").bitcast(F32)
+            nc.vector.tensor_copy(
+                out=fine_sorted[g, pair][:], in_=words.rearrange("p (s w u) -> p s u w", w=PART, u=2)
+            )
+
+        def turn_fine(g, pair):
+            for c in range(P_PASSES):
+                if pair == 0:
+                    fine_grouped[g, c] = staged("fine_grouped", [PART, SLOTS * K_PASS], BF16, 2 * P_PASSES)
+                bank = next_bank([PART, 2, 2 * PART])
+                for u in range(2):
+                    for j in range(2):
+                        nc.tensor.transpose(
+                            bank[:, u, j * PART : (j + 1) * PART], fine_sorted[g, pair][:, j * P_PASSES + c, u, :], ident[:]
+                        )
+                words = fine_grouped[g, c][:].bitcast(F32).rearrange("p (t pair q r u) -> p pair t q r u", t=SLOTS, pair=2, r=8, u=2)
+                nc.scalar.copy(out=words[:, pair], in_=bank[:].rearrange("p u (q t r) -> p t q r u", t=SLOTS, r=8))
+
+        def quantize_fine(g):
+            for c in range(P_PASSES):
+                fine_mx[g, c] = quantize("fine", fine_grouped[g, c], 2 * P_PASSES)
+
+        z_grouped, z_mx = {}, {}
+
+        def overlap_trial(g, b):
+            if b == 0:
+                z_grouped[g] = staged("z_grouped", [PART, SLOTS * B], BF16, 2)
+            cols = slice(b * PART, (b + 1) * PART)
+            bank = next_bank([PART, SLOTS, PART])
+            for t in range(SLOTS):
+                modes = slice(t * PART, (t + 1) * PART)
+                for c in range(P_PASSES):
+                    nc.tensor.matmul_mx(
+                        out=bank[:, t, :],
+                        lhsT=fine_mx[g, c][0][:, modes].bitcast(FP8X4),
+                        lhsT_scale=fine_mx[g, c][1][:, modes],
+                        rhs=trial_mx[c][0][:, cols].bitcast(FP8X4),
+                        rhs_scale=trial_mx[c][1][:, cols],
+                        start=(c == 0),
+                        stop=(c == P_PASSES - 1),
+                    )
+            nc.scalar.copy(
+                out=z_grouped[g][:].rearrange("p (n t) -> p n t", t=SLOTS)[:, cols, :],
+                in_=bank[:].rearrange("p t n -> p n t"),
+            )
+
+        def quantize_z(g):
+            z_mx[g] = quantize("z%d" % g, z_grouped[g], 0)
+
+        y_banks = {}
+
+        def admittance(a, groups):
+            if groups[0] == 0:
+                y_banks[a] = next_bank([PART, B])
+            half, tile_in_half = divmod(a, A_TILES // A_HALVES)
+            cols = slice(tile_in_half * PART, (tile_in_half + 1) * PART)
+            for g in groups:
+                nc.tensor.matmul_mx(
+                    out=y_banks[a][:],
+                    lhsT=v_mx[g, half][0][:, cols].bitcast(FP8X4),
+                    lhsT_scale=v_mx[g, half][1][:, cols],
+                    rhs=z_mx[g][0][:].bitcast(FP8X4),
+                    rhs_scale=z_mx[g][1][:],
+                    start=(g == 0),
+                    stop=(g == H_PASSES - 1),
+                )
+            if groups[-1] == H_PASSES - 1:
+                result = staged("result", [PART, B], F32, 4)
+                nc.vector.tensor_tensor(out=result[:], in0=y_banks[a][:], in1=y_ext_sb[:, a, :], op=ADD)
+                nc.sync.dma_start(out=out[a * PART : (a + 1) * PART, :], in_=result[:])
+
+        sort_modes(0)
+        spread_y_mode()
+        overlap_test(0, 0)
+        group_trial(0)
+        sort_modes(1)
+        sort_modes(2)
+        overlap_test(0, 1)
+        group_trial(1)
+        quantize_trial(0)
+        sort_fine(0, 0)
+        overlap_test(1, 0)
+        group_trial(2)
+        quantize_trial(1)
+        turn_fine(0, 0)
+        sort_fine(0, 1)
+        quantize_trial(2)
+        group_v(0, 0)
+        overlap_test(2, 0)
+        turn_fine(0, 1)
+        sort_fine(1, 0)
+        quantize_v(0, 0)
+        group_v(0, 1)
+        quantize_fine(0)
+        turn_fine(1, 0)
+        sort_fine(1, 1)
+        quantize_v(0, 1)
+        overlap_test(1, 1)
+        overlap_trial(0, 0)
+        overlap_trial(0, 1)
+        group_v(1, 0)
+        turn_fine(1, 1)
+        overlap_trial(0, 2)
+        overlap_trial(0, 3)
+        sort_fine(2, 0)
+        quantize_v(1, 0)
+        quantize_fine(1)
+        turn_fine(2, 0)
+        quantize_z(0)
+        sort_fine(2, 1)
+        group_v(2, 0)
+        overlap_test(2, 1)
+        overlap_trial(1, 0)
+        overlap_trial(1, 1)
+        quantize_v(2, 0)
+        turn_fine(2, 1)
+        group_v(1, 1)
+        overlap_trial(1, 2)
+        overlap_trial(1, 3)
+        quantize_fine(2)
+        quantize_v(1, 1)
+        quantize_z(1)
+        group_v(2, 1)
+        overlap_trial(2, 0)
+        overlap_trial(2, 1)
+        quantize_v(2, 1)
+        overlap_trial(2, 2)
+        overlap_trial(2, 3)
+        admittance(0, [0, 1])
+        admittance(1, [0, 1])
+        admittance(2, [0, 1])
+        quantize_z(2)
+        admittance(0, [2])
+        admittance(1, [2])
+        admittance(2, [2])
+        admittance(3, [0, 1, 2])
+        admittance(4, [0, 1, 2])
+        admittance(5, [0, 1, 2])
+        admittance(6, [0, 1, 2])
+        admittance(7, [0, 1, 2])

@@ -83,21 +83,23 @@ def tile_aperture_mode_admittance_s12_kernel(
         y_rows = kept("y_rows", [H_PASSES, K_PASS], BF16)
         y_sorted = kept("y_sorted", [PART, K_PASS], F32)
         y_cols = kept("y_cols", [PART, SLOTS, H_PASSES], F32)
+        zero = kept("zero", [PART, 1], F32)
         ident = kept("ident", [PART, PART], F32)
 
         nc.sync.dma_start(out=c_first[:].bitcast(I32), in_=c_words_hbm[:, :, :words_512])
         nc.sync.dma_start(out=d_codes[0][:].bitcast(I32), in_=d_words_hbm[:, :, :words_512])
         nc.scalar.dma_start(out=y_rows[:], in_=y_mode.rearrange("(g k) -> g k", g=H_PASSES))
+        nc.gpsimd.memset(zero[:], 0.0)
+        nc.scalar.activation(out=y_sorted[:], in_=zero[:].to_broadcast([PART, K_PASS]), func=COPY)
         nc.vector.memset(c_scales_raw[:].bitcast(I32), 0)
         nc.vector.memset(d_scales[:].bitcast(I32), 0)
-        nc.vector.memset(y_sorted[:], 0.0)
         make_identity(nc, ident[:])
         c_scales_hbm = mode_scales.bitcast(I32).rearrange("c (quad r) w -> r quad c w", r=4)
         d_scales_hbm = test_scales.bitcast(I32).rearrange("c (quad r) w -> r quad c w", r=4)
         for r in range(4):
             nc.sync.dma_start(out=c_scales_raw[r:PART:32].bitcast(I32), in_=c_scales_hbm[r])
         for r in range(4):
-            nc.scalar.dma_start(out=d_scales[r:PART:32].bitcast(I32), in_=d_scales_hbm[r])
+            nc.sync.dma_start(out=d_scales[r:PART:32].bitcast(I32), in_=d_scales_hbm[r])
 
         trial_rows = [kept("trial_rows%d" % c, [PART, SLOTS, B], BF16) for c in range(P_PASSES)]
         fine_rows = {}
@@ -147,9 +149,10 @@ def tile_aperture_mode_admittance_s12_kernel(
             )
 
         def spread_y_mode():
-            nc.scalar.copy(
+            nc.scalar.activation(
                 out=y_sorted[:H_PASSES].rearrange("g (t q r) -> g t q r", t=SLOTS, r=8),
                 in_=y_rows[:].rearrange("g (q t r) -> g t q r", t=SLOTS, r=8),
+                func=COPY,
             )
             bank = next_bank([PART, SLOTS, PART])
             for t in range(SLOTS):
@@ -243,25 +246,26 @@ def tile_aperture_mode_admittance_s12_kernel(
 
         y_banks = {}
 
-        def admittance(a, groups):
+        def admittance(a, groups, cols=slice(0, B)):
+            width = cols.stop - cols.start
             if groups[0] == 0:
-                y_banks[a] = next_bank([PART, B])
+                y_banks[a] = next_bank([PART, width])
             half, tile_in_half = divmod(a, A_TILES // A_HALVES)
-            cols = slice(tile_in_half * PART, (tile_in_half + 1) * PART)
+            rows = slice(tile_in_half * PART, (tile_in_half + 1) * PART)
             for g in groups:
                 nc.tensor.matmul_mx(
                     out=y_banks[a][:],
-                    lhsT=v_mx[g, half][0][:, cols].bitcast(FP8X4),
-                    lhsT_scale=v_mx[g, half][1][:, cols],
-                    rhs=z_mx[g][0][:].bitcast(FP8X4),
-                    rhs_scale=z_mx[g][1][:],
+                    lhsT=v_mx[g, half][0][:, rows].bitcast(FP8X4),
+                    lhsT_scale=v_mx[g, half][1][:, rows],
+                    rhs=z_mx[g][0][:, cols].bitcast(FP8X4),
+                    rhs_scale=z_mx[g][1][:, cols],
                     start=(g == 0),
                     stop=(g == H_PASSES - 1),
                 )
             if groups[-1] == H_PASSES - 1:
-                result = staged("result", [PART, B], F32, 4)
-                nc.vector.tensor_tensor(out=result[:], in0=y_banks[a][:], in1=y_ext_sb[:, a, :], op=ADD)
-                nc.sync.dma_start(out=out[a * PART : (a + 1) * PART, :], in_=result[:])
+                result = staged("result", [PART, width], F32, 6)
+                nc.vector.tensor_tensor(out=result[:], in0=y_banks[a][:], in1=y_ext_sb[:, a, cols], op=ADD)
+                nc.sync.dma_start(out=out[a * PART : (a + 1) * PART, cols], in_=result[:])
 
         sort_modes(0)
         spread_y_mode()
@@ -271,64 +275,66 @@ def tile_aperture_mode_admittance_s12_kernel(
         sort_modes(2)
         overlap_test(0, 1)
         group_trial(1)
-        quantize_trial(0)
         sort_fine(0, 0)
+        quantize_trial(0)
         overlap_test(1, 0)
-        group_trial(2)
-        quantize_trial(1)
-        turn_fine(0, 0)
         sort_fine(0, 1)
-        quantize_trial(2)
-        group_v(0, 0)
-        overlap_test(2, 0)
+        group_trial(2)
+        turn_fine(0, 0)
+        quantize_trial(1)
         turn_fine(0, 1)
+        quantize_trial(2)
+        overlap_test(2, 0)
         sort_fine(1, 0)
-        quantize_v(0, 0)
-        group_v(0, 1)
         quantize_fine(0)
         turn_fine(1, 0)
         sort_fine(1, 1)
-        quantize_v(0, 1)
-        overlap_test(1, 1)
+        group_v(0, 0)
         overlap_trial(0, 0)
-        overlap_trial(0, 1)
-        group_v(1, 0)
+        quantize_v(0, 0)
         turn_fine(1, 1)
-        overlap_trial(0, 2)
-        overlap_trial(0, 3)
+        overlap_trial(0, 1)
+        group_v(0, 1)
         sort_fine(2, 0)
-        quantize_v(1, 0)
+        overlap_trial(0, 2)
         quantize_fine(1)
+        overlap_trial(0, 3)
+        quantize_v(0, 1)
         turn_fine(2, 0)
-        quantize_z(0)
         sort_fine(2, 1)
-        group_v(2, 0)
-        overlap_test(2, 1)
+        quantize_z(0)
+        overlap_test(1, 1)
+        group_v(1, 0)
         overlap_trial(1, 0)
-        overlap_trial(1, 1)
-        quantize_v(2, 0)
+        quantize_v(1, 0)
         turn_fine(2, 1)
-        group_v(1, 1)
+        overlap_trial(1, 1)
+        group_v(2, 0)
         overlap_trial(1, 2)
-        overlap_trial(1, 3)
         quantize_fine(2)
-        quantize_v(1, 1)
-        quantize_z(1)
-        group_v(2, 1)
+        overlap_trial(1, 3)
+        quantize_v(2, 0)
+        overlap_test(2, 1)
+        group_v(1, 1)
         overlap_trial(2, 0)
+        quantize_z(1)
+        quantize_v(1, 1)
         overlap_trial(2, 1)
-        quantize_v(2, 1)
+        group_v(2, 1)
         overlap_trial(2, 2)
         overlap_trial(2, 3)
+        quantize_v(2, 1)
         admittance(0, [0, 1])
         admittance(1, [0, 1])
         admittance(2, [0, 1])
+        admittance(3, [0, 1])
         quantize_z(2)
         admittance(0, [2])
         admittance(1, [2])
         admittance(2, [2])
-        admittance(3, [0, 1, 2])
+        admittance(3, [2])
         admittance(4, [0, 1, 2])
         admittance(5, [0, 1, 2])
         admittance(6, [0, 1, 2])
-        admittance(7, [0, 1, 2])
+        admittance(7, [0, 1, 2], slice(0, B // 2))
+        admittance(7, [0, 1, 2], slice(B // 2, B))

@@ -78,7 +78,8 @@ def tile_aperture_mode_admittance_s12_kernel(
         c_first = kept("c_first", [PART, Q_PASSES, 2 * K_PASS], U8)
         c_rest = kept("c_rest", [PART, Q_PASSES, 2 * (H - K_PASS)], U8)
         d_codes = [kept("d_codes%d" % half, [PART, Q_PASSES, 2 * BANK], U8) for half in range(A_HALVES)]
-        c_scales_raw = kept("c_scales_raw", [PART, Q_PASSES, H], U8)
+        c_first_scales = kept("c_first_scales", [PART, Q_PASSES, K_PASS], U8)
+        c_rest_scales = kept("c_rest_scales", [PART, Q_PASSES, H - K_PASS], U8)
         d_scales = kept("d_scales", [PART, Q_PASSES, A], U8)
         y_rows = kept("y_rows", [H_PASSES, K_PASS], BF16)
         y_sorted = kept("y_sorted", [PART, K_PASS], F32)
@@ -91,13 +92,13 @@ def tile_aperture_mode_admittance_s12_kernel(
         nc.scalar.dma_start(out=y_rows[:], in_=y_mode.rearrange("(g k) -> g k", g=H_PASSES))
         nc.gpsimd.memset(zero[:], 0.0)
         nc.scalar.activation(out=y_sorted[:], in_=zero[:].to_broadcast([PART, K_PASS]), func=COPY)
-        nc.vector.memset(c_scales_raw[:].bitcast(I32), 0)
-        nc.vector.memset(d_scales[:].bitcast(I32), 0)
+        for plane in (c_first_scales, d_scales, c_rest_scales):
+            nc.vector.memset(plane[:].bitcast(I32), 0)
         make_identity(nc, ident[:])
         c_scales_hbm = mode_scales.bitcast(I32).rearrange("c (quad r) w -> r quad c w", r=4)
         d_scales_hbm = test_scales.bitcast(I32).rearrange("c (quad r) w -> r quad c w", r=4)
         for r in range(4):
-            nc.sync.dma_start(out=c_scales_raw[r:PART:32].bitcast(I32), in_=c_scales_hbm[r])
+            nc.sync.dma_start(out=c_first_scales[r:PART:32].bitcast(I32), in_=c_scales_hbm[r][:, :, :PART])
         for r in range(4):
             nc.sync.dma_start(out=d_scales[r:PART:32].bitcast(I32), in_=d_scales_hbm[r])
 
@@ -120,6 +121,8 @@ def tile_aperture_mode_admittance_s12_kernel(
         load_trial(0)
         nc.sync.dma_start(out=d_codes[1][:].bitcast(I32), in_=d_words_hbm[:, :, words_512:])
         nc.sync.dma_start(out=c_rest[:].bitcast(I32), in_=c_words_hbm[:, :, words_512:])
+        for r in range(4):
+            nc.sync.dma_start(out=c_rest_scales[r:PART:32].bitcast(I32), in_=c_scales_hbm[r][:, :, PART:])
         load_trial(1)
         load_fine(0, 0)
         load_trial(2)
@@ -131,22 +134,20 @@ def tile_aperture_mode_admittance_s12_kernel(
 
         c_codes, c_scales = {}, {}
 
-        def sort_modes(g):
-            if g == 0:
-                words = c_first[:].bitcast(I32)
-            else:
-                words = c_rest[:].bitcast(I32)[:, :, (g - 1) * words_512 : g * words_512]
-            c_codes[g] = kept("c_codes%d" % g, [PART, Q_PASSES, SLOTS, 2 * PART], U8)
-            c_scales[g] = kept("c_scales%d" % g, [PART, Q_PASSES, SLOTS, PART], U8)
-            nc.vector.tensor_copy(
-                out=c_codes[g][:].bitcast(I32).rearrange("p c t (q w) -> p c t q w", w=4),
-                in_=words.rearrange("p c (q t w) -> p c t q w", t=SLOTS, w=4),
-            )
-            scale_words = c_scales_raw[:].bitcast(I32)[:, :, g * PART : (g + 1) * PART]
-            nc.vector.tensor_copy(
-                out=c_scales[g][:].bitcast(I32).rearrange("p c t (q w) -> p c t q w", w=2),
-                in_=scale_words.rearrange("p c (q t w) -> p c t q w", t=SLOTS, w=2),
-            )
+        def sort_modes(name, words, scales, groups):
+            count = Q_PASSES * len(groups)
+            sorted_words = kept(name + "_sorted", [PART, count, SLOTS, 2 * PART], U8)
+            sorted_scales = kept(name + "_sorted_scales", [PART, count, SLOTS, PART], U8)
+            for dst, src, run in ((sorted_words, words, 4), (sorted_scales, scales, 2)):
+                flat = src[:].rearrange("p c n -> p (c n)").bitcast(I32)
+                nc.vector.tensor_copy(
+                    out=dst[:].bitcast(I32).rearrange("p s t (q w) -> p s t q w", w=run),
+                    in_=flat.rearrange("p (s q t w) -> p s t q w", s=count, t=SLOTS, w=run),
+                )
+            for n, g in enumerate(groups):
+                for c in range(Q_PASSES):
+                    c_codes[g, c] = sorted_words[:, c * len(groups) + n]
+                    c_scales[g, c] = sorted_scales[:, c * len(groups) + n]
 
         def spread_y_mode():
             nc.scalar.activation(
@@ -161,15 +162,16 @@ def tile_aperture_mode_admittance_s12_kernel(
 
         v_rows, v_grouped, v_mx = {}, {}, {}
 
-        def overlap_test(g, half):
-            v_rows[g, half] = staged("v_rows", [PART, SLOTS, BANK], BF16, 4)
-            for t in range(SLOTS):
+        def overlap_test(g, half, slots=range(SLOTS)):
+            if slots[0] == 0:
+                v_rows[g, half] = staged("v_rows", [PART, SLOTS, BANK], BF16, 4)
+            for t in slots:
                 bank = next_bank([PART, BANK])
                 for c in range(Q_PASSES):
                     nc.tensor.matmul_mx(
                         out=bank[:],
-                        lhsT=c_codes[g][:, c, t, :].bitcast(FP4X4),
-                        lhsT_scale=c_scales[g][:, c, t, :],
+                        lhsT=c_codes[g, c][:, t, :].bitcast(FP4X4),
+                        lhsT_scale=c_scales[g, c][:, t, :],
                         rhs=d_codes[half][:, c, :].bitcast(FP4X4),
                         rhs_scale=d_scales[:, c, half * BANK : (half + 1) * BANK],
                         start=(c == 0),
@@ -207,9 +209,12 @@ def tile_aperture_mode_admittance_s12_kernel(
                 bank = next_bank([PART, 2, 2 * PART])
                 for u in range(2):
                     for j in range(2):
-                        nc.tensor.transpose(
-                            bank[:, u, j * PART : (j + 1) * PART], fine_sorted[g, pair][:, j * P_PASSES + c, u, :], ident[:]
-                        )
+                        if (g, pair) in fine_sorted:
+                            source = fine_sorted[g, pair][:, j * P_PASSES + c, u, :]
+                        else:
+                            row_words = fine_rows[g, pair][:, j, :].bitcast(F32)
+                            source = row_words[:, 2 * PART * c + u : 2 * PART * (c + 1) : 2]
+                        nc.tensor.transpose(bank[:, u, j * PART : (j + 1) * PART], source, ident[:])
                 words = fine_grouped[g, c][:].bitcast(F32).rearrange("p (t pair q r u) -> p pair t q r u", t=SLOTS, pair=2, r=8, u=2)
                 nc.scalar.copy(out=words[:, pair], in_=bank[:].rearrange("p u (q t r) -> p t q r u", t=SLOTS, r=8))
 
@@ -267,23 +272,21 @@ def tile_aperture_mode_admittance_s12_kernel(
                 nc.vector.tensor_tensor(out=result[:], in0=y_banks[a][:], in1=y_ext_sb[:, a, cols], op=ADD)
                 nc.sync.dma_start(out=out[a * PART : (a + 1) * PART, cols], in_=result[:])
 
-        sort_modes(0)
+        sort_modes("c_first", c_first, c_first_scales, [0])
         spread_y_mode()
         overlap_test(0, 0)
         group_trial(0)
-        sort_modes(1)
-        sort_modes(2)
+        sort_modes("c_rest", c_rest, c_rest_scales, [1, 2])
         overlap_test(0, 1)
         group_trial(1)
-        sort_fine(0, 0)
         quantize_trial(0)
-        overlap_test(1, 0)
-        sort_fine(0, 1)
+        overlap_test(1, 0, range(0, 2))
         group_trial(2)
         turn_fine(0, 0)
+        overlap_test(1, 0, range(2, 4))
         quantize_trial(1)
-        turn_fine(0, 1)
         quantize_trial(2)
+        turn_fine(0, 1)
         overlap_test(2, 0)
         sort_fine(1, 0)
         quantize_fine(0)

@@ -87,18 +87,19 @@ def tile_aperture_mode_admittance_s12_kernel(
         zero = kept("zero", [PART, 1], F32)
         ident = kept("ident", [PART, PART], F32)
 
-        nc.sync.dma_start(out=c_first[:].bitcast(I32), in_=c_words_hbm[:, :, :words_512])
-        nc.sync.dma_start(out=d_codes[0][:].bitcast(I32), in_=d_words_hbm[:, :, :words_512])
-        nc.scalar.dma_start(out=y_rows[:], in_=y_mode.rearrange("(g k) -> g k", g=H_PASSES))
-        nc.gpsimd.memset(zero[:], 0.0)
-        nc.scalar.activation(out=y_sorted[:], in_=zero[:].to_broadcast([PART, K_PASS]), func=COPY)
-        for plane in (c_first_scales, d_scales, c_rest_scales):
-            nc.vector.memset(plane[:].bitcast(I32), 0)
-        make_identity(nc, ident[:])
         c_scales_hbm = mode_scales.bitcast(I32).rearrange("c (quad r) w -> r quad c w", r=4)
         d_scales_hbm = test_scales.bitcast(I32).rearrange("c (quad r) w -> r quad c w", r=4)
+        nc.gpsimd.memset(c_first_scales[:].bitcast(I32), 0)
+        nc.gpsimd.memset(zero[:], 0.0)
+        nc.sync.dma_start(out=c_first[:].bitcast(I32), in_=c_words_hbm[:, :, :words_512])
+        nc.scalar.dma_start(out=y_rows[:], in_=y_mode.rearrange("(g k) -> g k", g=H_PASSES))
+        nc.scalar.activation(out=y_sorted[:], in_=zero[:].to_broadcast([PART, K_PASS]), func=COPY)
+        for plane in (d_scales, c_rest_scales):
+            nc.vector.memset(plane[:].bitcast(I32), 0)
+        make_identity(nc, ident[:])
         for r in range(4):
             nc.sync.dma_start(out=c_first_scales[r:PART:32].bitcast(I32), in_=c_scales_hbm[r][:, :, :PART])
+        nc.sync.dma_start(out=d_codes[0][:].bitcast(I32), in_=d_words_hbm[:, :, :words_512])
         for r in range(4):
             nc.sync.dma_start(out=d_scales[r:PART:32].bitcast(I32), in_=d_scales_hbm[r])
 
@@ -119,7 +120,6 @@ def tile_aperture_mode_admittance_s12_kernel(
             nc.sync.dma_start(out=fine_rows[g, pair][:], in_=rows.rearrange("(j p) k -> p j k", p=PART))
 
         load_trial(0)
-        nc.sync.dma_start(out=d_codes[1][:].bitcast(I32), in_=d_words_hbm[:, :, words_512:])
         nc.sync.dma_start(out=c_rest[:].bitcast(I32), in_=c_words_hbm[:, :, words_512:])
         for r in range(4):
             nc.sync.dma_start(out=c_rest_scales[r:PART:32].bitcast(I32), in_=c_scales_hbm[r][:, :, PART:])
@@ -127,6 +127,7 @@ def tile_aperture_mode_admittance_s12_kernel(
         load_fine(0, 0)
         load_trial(2)
         load_fine(0, 1)
+        nc.sync.dma_start(out=d_codes[1][:].bitcast(I32), in_=d_words_hbm[:, :, words_512:])
         for g in range(1, H_PASSES):
             for pair in range(ROW_PAIRS):
                 load_fine(g, pair)
@@ -246,98 +247,100 @@ def tile_aperture_mode_admittance_s12_kernel(
                 in_=bank[:].rearrange("p t n -> p n t"),
             )
 
-        def quantize_z(g):
-            z_mx[g] = quantize("z%d" % g, z_grouped[g], 0)
+        def quantize_z(g, cols):
+            if cols.start == 0:
+                z_mx[g] = (kept("z%d_codes" % g, [PART, B], U32), kept("z%d_scales" % g, [PART, B], U8))
+            codes, scales = z_mx[g]
+            values = z_grouped[g][:, SLOTS * cols.start : SLOTS * cols.stop]
+            nc.vector.quantize_mx(out=codes[:, cols].bitcast(FP8X4), scales=scales[:, cols], in_=values)
 
-        y_banks = {}
-
-        def admittance(a, groups, cols=slice(0, B)):
+        def admittance(first, count, cols):
             width = cols.stop - cols.start
-            if groups[0] == 0:
-                y_banks[a] = next_bank([PART, width])
-            half, tile_in_half = divmod(a, A_TILES // A_HALVES)
-            rows = slice(tile_in_half * PART, (tile_in_half + 1) * PART)
-            for g in groups:
-                nc.tensor.matmul_mx(
-                    out=y_banks[a][:],
-                    lhsT=v_mx[g, half][0][:, rows].bitcast(FP8X4),
-                    lhsT_scale=v_mx[g, half][1][:, rows],
-                    rhs=z_mx[g][0][:, cols].bitcast(FP8X4),
-                    rhs_scale=z_mx[g][1][:, cols],
-                    start=(g == 0),
-                    stop=(g == H_PASSES - 1),
-                )
-            if groups[-1] == H_PASSES - 1:
-                result = staged("result", [PART, width], F32, 6)
-                nc.vector.tensor_tensor(out=result[:], in0=y_banks[a][:], in1=y_ext_sb[:, a, cols], op=ADD)
-                nc.sync.dma_start(out=out[a * PART : (a + 1) * PART, cols], in_=result[:])
+            bank = next_bank([PART, count, width])
+            for n in range(count):
+                half, tile_in_half = divmod(first + n, A_TILES // A_HALVES)
+                rows = slice(tile_in_half * PART, (tile_in_half + 1) * PART)
+                for g in range(H_PASSES):
+                    nc.tensor.matmul_mx(
+                        out=bank[:, n, :],
+                        lhsT=v_mx[g, half][0][:, rows].bitcast(FP8X4),
+                        lhsT_scale=v_mx[g, half][1][:, rows],
+                        rhs=z_mx[g][0][:, cols].bitcast(FP8X4),
+                        rhs_scale=z_mx[g][1][:, cols],
+                        start=(g == 0),
+                        stop=(g == H_PASSES - 1),
+                    )
+            result = staged("result", [PART, count, width], F32, 6)
+            nc.vector.tensor_tensor(out=result[:], in0=bank[:], in1=y_ext_sb[:, first : first + count, cols], op=ADD)
+            rows_out = out[first * PART : (first + count) * PART, cols]
+            nc.sync.dma_start(out=rows_out.rearrange("(n p) b -> p n b", p=PART), in_=result[:])
 
+        left, right, whole = slice(0, B // 2), slice(B // 2, B), slice(0, B)
         sort_modes("c_first", c_first, c_first_scales, [0])
         spread_y_mode()
         overlap_test(0, 0)
         group_trial(0)
         sort_modes("c_rest", c_rest, c_rest_scales, [1, 2])
-        overlap_test(0, 1)
+        overlap_test(1, 0)
         group_trial(1)
+        sort_fine(0, 0)
         quantize_trial(0)
-        overlap_test(1, 0, range(0, 2))
+        overlap_test(2, 0, range(0, 2))
         group_trial(2)
         turn_fine(0, 0)
-        overlap_test(1, 0, range(2, 4))
+        overlap_test(2, 0, range(2, 4))
+        sort_fine(0, 1)
         quantize_trial(1)
         quantize_trial(2)
         turn_fine(0, 1)
-        overlap_test(2, 0)
+        overlap_test(0, 1)
         sort_fine(1, 0)
         quantize_fine(0)
         turn_fine(1, 0)
         sort_fine(1, 1)
         group_v(0, 0)
         overlap_trial(0, 0)
-        quantize_v(0, 0)
-        turn_fine(1, 1)
-        overlap_trial(0, 1)
-        group_v(0, 1)
         sort_fine(2, 0)
+        turn_fine(1, 1)
+        quantize_v(0, 0)
+        overlap_trial(0, 1)
+        group_v(1, 0)
         overlap_trial(0, 2)
         quantize_fine(1)
         overlap_trial(0, 3)
-        quantize_v(0, 1)
+        quantize_v(1, 0)
         turn_fine(2, 0)
         sort_fine(2, 1)
-        quantize_z(0)
+        group_v(2, 0)
         overlap_test(1, 1)
-        group_v(1, 0)
+        quantize_z(0, whole)
         overlap_trial(1, 0)
-        quantize_v(1, 0)
+        quantize_v(2, 0)
         turn_fine(2, 1)
         overlap_trial(1, 1)
-        group_v(2, 0)
+        group_v(0, 1)
         overlap_trial(1, 2)
         quantize_fine(2)
         overlap_trial(1, 3)
-        quantize_v(2, 0)
+        quantize_v(0, 1)
         overlap_test(2, 1)
         group_v(1, 1)
         overlap_trial(2, 0)
-        quantize_z(1)
-        quantize_v(1, 1)
+        quantize_z(1, whole)
         overlap_trial(2, 1)
-        group_v(2, 1)
+        quantize_v(1, 1)
+        quantize_z(2, left)
         overlap_trial(2, 2)
+        group_v(2, 1)
         overlap_trial(2, 3)
+        quantize_z(2, right)
+        admittance(0, 2, left)
         quantize_v(2, 1)
-        admittance(0, [0, 1])
-        admittance(1, [0, 1])
-        admittance(2, [0, 1])
-        admittance(3, [0, 1])
-        quantize_z(2)
-        admittance(0, [2])
-        admittance(1, [2])
-        admittance(2, [2])
-        admittance(3, [2])
-        admittance(4, [0, 1, 2])
-        admittance(5, [0, 1, 2])
-        admittance(6, [0, 1, 2])
-        admittance(7, [0, 1, 2], slice(0, B // 2))
-        admittance(7, [0, 1, 2], slice(B // 2, B))
+        admittance(2, 2, left)
+        admittance(0, 2, right)
+        admittance(2, 2, right)
+        admittance(4, 2, left)
+        admittance(6, 2, left)
+        admittance(4, 2, right)
+        admittance(6, 1, right)
+        admittance(7, 1, right)

from contextlib import ExitStack

import concourse.mybir as mybir
from concourse.masks import make_identity

Q, P, H, A, B = 1024, 1536, 1536, 1024, 512
FLOPS = 2 * (Q * H * A + H * P * B + H * A * B)

F32 = mybir.dt.float32
BF16 = mybir.dt.bfloat16
I32 = mybir.dt.int32
U32 = mybir.dt.uint32
U8 = mybir.dt.uint8
FP8X4 = mybir.dt.float8_e4m3fn_x4
FP4X4 = mybir.dt.float4_e2m1fn_x4
COPY = mybir.ActivationFunctionType.Copy
ADD = mybir.AluOpType.add

PART = 128
SLOTS = 4
K_PASS = PART * SLOTS
BANK = 512
BANKS = 8
Q_PASSES = Q // K_PASS
P_PASSES = P // K_PASS
H_PASSES = H // K_PASS
A_HALVES = A // BANK
A_TILES = A // PART
B_TILES = B // PART
ROW_PAIRS = 2


def tile_aperture_mode_admittance_s12_kernel(
    tc, mode_words, mode_scales, test_words, test_scales, fine_modes, trial, y_mode, y_ext, out
):
    nc = tc.nc
    with ExitStack() as ctx:
        keep = ctx.enter_context(tc.tile_pool(name="keep", bufs=1))
        ring = ctx.enter_context(tc.tile_pool(name="ring", bufs=2))
        psum = ctx.enter_context(tc.psum_pool(name="psum", bufs=1))
        ctx.enter_context(tc.manual_schedule())

        def kept(name, shape, dtype):
            return keep.tile(shape, dtype, name=name, align_bytes=64)

        def staged(name, shape, dtype, bufs):
            return ring.tile(shape, dtype, name=name, tag=name, bufs=bufs, align_bytes=64)

        taken = []

        def next_bank(shape):
            name = "bank%d" % (len(taken) % BANKS)
            taken.append(name)
            return psum.tile(shape, F32, name=name, tag=name)

        def quantize(name, grouped, bufs):
            if bufs:
                codes = staged(name + "_codes", [PART, K_PASS], U32, bufs)
                scales = staged(name + "_scales", [PART, K_PASS], U8, bufs)
            else:
                codes = kept(name + "_codes", [PART, K_PASS], U32)
                scales = kept(name + "_scales", [PART, K_PASS], U8)
            nc.vector.quantize_mx(out=codes[:].bitcast(FP8X4), scales=scales[:], in_=grouped[:])
            return codes, scales

        def interleave(name, rows):
            grouped = staged(name, [PART, SLOTS * BANK], BF16, 2)
            nc.vector.tensor_copy(
                out=grouped[:].rearrange("p (n i t) -> p n t i", i=4, t=SLOTS),
                in_=rows[:].rearrange("p t (n i) -> p n t i", i=4),
            )
            return grouped

        c_words_hbm = mode_words.bitcast(I32).rearrange("c p w -> p c w")
        d_words_hbm = test_words.bitcast(I32).rearrange("c p w -> p c w")
        words_512 = K_PASS * 2 // 4

        c_first = kept("c_first", [PART, Q_PASSES, 2 * K_PASS], U8)
        c_rest = kept("c_rest", [PART, Q_PASSES, 2 * (H - K_PASS)], U8)
        d_codes = [kept("d_codes%d" % half, [PART, Q_PASSES, 2 * BANK], U8) for half in range(A_HALVES)]
        c_first_scales = kept("c_first_scales", [PART, Q_PASSES, K_PASS], U8)
        c_rest_scales = kept("c_rest_scales", [PART, Q_PASSES, H - K_PASS], U8)
        d_scales = kept("d_scales", [PART, Q_PASSES, A], U8)
        y_rows = kept("y_rows", [H_PASSES, K_PASS], BF16)
        y_sorted = kept("y_sorted", [PART, K_PASS], F32)
        y_cols = kept("y_cols", [PART, SLOTS, H_PASSES], F32)
        zero = kept("zero", [PART, 1], F32)
        ident = kept("ident", [PART, PART], F32)

        c_scales_hbm = mode_scales.bitcast(I32).rearrange("c (quad r) w -> r quad c w", r=4)
        d_scales_hbm = test_scales.bitcast(I32).rearrange("c (quad r) w -> r quad c w", r=4)
        nc.gpsimd.memset(c_first_scales[:].bitcast(I32), 0)
        nc.gpsimd.memset(zero[:], 0.0)
        nc.sync.dma_start(out=c_first[:].bitcast(I32), in_=c_words_hbm[:, :, :words_512])
        nc.scalar.dma_start(out=y_rows[:], in_=y_mode.rearrange("(g k) -> g k", g=H_PASSES))
        nc.scalar.activation(out=y_sorted[:], in_=zero[:].to_broadcast([PART, K_PASS]), func=COPY)
        for plane in (d_scales, c_rest_scales):
            nc.vector.memset(plane[:].bitcast(I32), 0)
        make_identity(nc, ident[:])
        for r in range(4):
            nc.sync.dma_start(out=c_first_scales[r:PART:32].bitcast(I32), in_=c_scales_hbm[r][:, :, :PART])
        nc.sync.dma_start(out=d_codes[0][:].bitcast(I32), in_=d_words_hbm[:, :, :words_512])
        for r in range(4):
            nc.sync.dma_start(out=d_scales[r:PART:32].bitcast(I32), in_=d_scales_hbm[r])

        trial_rows = [kept("trial_rows%d" % c, [PART, SLOTS, B], BF16) for c in range(P_PASSES)]
        fine_rows = {}
        for g in range(H_PASSES):
            for pair in range(ROW_PAIRS):
                fine_rows[g, pair] = kept("fine_rows%d%d" % (g, pair), [PART, 2, P], BF16)
        y_ext_sb = kept("y_ext_sb", [PART, A_TILES, B], BF16)

        def load_trial(c):
            rows = trial[c * K_PASS : (c + 1) * K_PASS, :]
            nc.sync.dma_start(out=trial_rows[c][:], in_=rows.rearrange("(p t) n -> p t n", t=SLOTS))

        def load_fine(g, pair):
            first = g * K_PASS + pair * 2 * PART
            rows = fine_modes[first : first + 2 * PART, :]
            nc.sync.dma_start(out=fine_rows[g, pair][:], in_=rows.rearrange("(j p) k -> p j k", p=PART))

        load_trial(0)
        nc.sync.dma_start(out=c_rest[:].bitcast(I32), in_=c_words_hbm[:, :, words_512:])
        for r in range(4):
            nc.sync.dma_start(out=c_rest_scales[r:PART:32].bitcast(I32), in_=c_scales_hbm[r][:, :, PART:])
        load_trial(1)
        load_fine(0, 0)
        load_trial(2)
        load_fine(0, 1)
        nc.sync.dma_start(out=d_codes[1][:].bitcast(I32), in_=d_words_hbm[:, :, words_512:])
        for g in range(1, H_PASSES):
            for pair in range(ROW_PAIRS):
                load_fine(g, pair)
        nc.sync.dma_start(out=y_ext_sb[:], in_=y_ext.rearrange("(a p) n -> p a n", p=PART))

        c_codes, c_scales = {}, {}

        def sort_modes(name, words, scales, groups):
            count = Q_PASSES * len(groups)
            sorted_words = kept(name + "_sorted", [PART, count, SLOTS, 2 * PART], U8)
            sorted_scales = kept(name + "_sorted_scales", [PART, count, SLOTS, PART], U8)
            for dst, src, run in ((sorted_words, words, 4), (sorted_scales, scales, 2)):
                flat = src[:].rearrange("p c n -> p (c n)").bitcast(I32)
                nc.vector.tensor_copy(
                    out=dst[:].bitcast(I32).rearrange("p s t (q w) -> p s t q w", w=run),
                    in_=flat.rearrange("p (s q t w) -> p s t q w", s=count, t=SLOTS, w=run),
                )
            for n, g in enumerate(groups):
                for c in range(Q_PASSES):
                    c_codes[g, c] = sorted_words[:, c * len(groups) + n]
                    c_scales[g, c] = sorted_scales[:, c * len(groups) + n]

        def spread_y_mode():
            nc.scalar.activation(
                out=y_sorted[:H_PASSES].rearrange("g (t q r) -> g t q r", t=SLOTS, r=8),
                in_=y_rows[:].rearrange("g (q t r) -> g t q r", t=SLOTS, r=8),
                func=COPY,
            )
            bank = next_bank([PART, SLOTS, PART])
            for t in range(SLOTS):
                nc.tensor.transpose(bank[:, t, :], y_sorted[:, t * PART : (t + 1) * PART], ident[:])
            nc.scalar.copy(out=y_cols[:], in_=bank[:, :, :H_PASSES])

        v_rows, v_grouped, v_mx = {}, {}, {}

        def overlap_test(g, half, slots=range(SLOTS)):
            if slots[0] == 0:
                v_rows[g, half] = staged("v_rows", [PART, SLOTS, BANK], BF16, 4)
            for t in slots:
                bank = next_bank([PART, BANK])
                for c in range(Q_PASSES):
                    nc.tensor.matmul_mx(
                        out=bank[:],
                        lhsT=c_codes[g, c][:, t, :].bitcast(FP4X4),
                        lhsT_scale=c_scales[g, c][:, t, :],
                        rhs=d_codes[half][:, c, :].bitcast(FP4X4),
                        rhs_scale=d_scales[:, c, half * BANK : (half + 1) * BANK],
                        start=(c == 0),
                        stop=(c == Q_PASSES - 1),
                    )
                nc.scalar.activation(out=v_rows[g, half][:, t, :], in_=bank[:], func=COPY, scale=y_cols[:, t, g : g + 1])

        def group_v(g, half):
            v_grouped[g, half] = interleave("v_grouped", v_rows[g, half])

        def quantize_v(g, half):
            v_mx[g, half] = quantize("v%d%d" % (g, half), v_grouped[g, half], 0)

        trial_grouped, trial_mx = {}, {}

        def group_trial(c):
            trial_grouped[c] = interleave("trial_grouped", trial_rows[c])

        def quantize_trial(c):
            trial_mx[c] = quantize("trial%d" % c, trial_grouped[c], 0)

        fine_sorted, fine_grouped, fine_mx = {}, {}, {}

        def sort_fine(g, pair):
            fine_sorted[g, pair] = staged("fine_sorted", [PART, 2 * P_PASSES, 2, PART], F32, 3)
            words = fine_rows[g, pair][:].rearrange("p j k -> p (j k)").bitcast(F32)
            nc.vector.tensor_copy(
                out=fine_sorted[g, pair][:], in_=words.rearrange("p (s w u) -> p s u w", w=PART, u=2)
            )

        def turn_fine(g, pair):
            for c in range(P_PASSES):
                if pair == 0:
                    fine_grouped[g, c] = staged("fine_grouped", [PART, SLOTS * K_PASS], BF16, 2 * P_PASSES)
                bank = next_bank([PART, 2, 2 * PART])
                for u in range(2):
                    for j in range(2):
                        if (g, pair) in fine_sorted:
                            source = fine_sorted[g, pair][:, j * P_PASSES + c, u, :]
                        else:
                            row_words = fine_rows[g, pair][:, j, :].bitcast(F32)
                            source = row_words[:, 2 * PART * c + u : 2 * PART * (c + 1) : 2]
                        nc.tensor.transpose(bank[:, u, j * PART : (j + 1) * PART], source, ident[:])
                words = fine_grouped[g, c][:].bitcast(F32).rearrange("p (t pair q r u) -> p pair t q r u", t=SLOTS, pair=2, r=8, u=2)
                nc.scalar.copy(out=words[:, pair], in_=bank[:].rearrange("p u (q t r) -> p t q r u", t=SLOTS, r=8))

        def quantize_fine(g):
            for c in range(P_PASSES):
                fine_mx[g, c] = quantize("fine", fine_grouped[g, c], 2 * P_PASSES)

        z_grouped, z_mx = {}, {}

        def overlap_trial(g, b):
            if b == 0:
                z_grouped[g] = staged("z_grouped", [PART, SLOTS * B], BF16, 2)
            cols = slice(b * PART, (b + 1) * PART)
            bank = next_bank([PART, SLOTS, PART])
            for t in range(SLOTS):
                modes = slice(t * PART, (t + 1) * PART)
                for c in range(P_PASSES):
                    nc.tensor.matmul_mx(
                        out=bank[:, t, :],
                        lhsT=fine_mx[g, c][0][:, modes].bitcast(FP8X4),
                        lhsT_scale=fine_mx[g, c][1][:, modes],
                        rhs=trial_mx[c][0][:, cols].bitcast(FP8X4),
                        rhs_scale=trial_mx[c][1][:, cols],
                        start=(c == 0),
                        stop=(c == P_PASSES - 1),
                    )
            nc.scalar.copy(
                out=z_grouped[g][:].rearrange("p (n t) -> p n t", t=SLOTS)[:, cols, :],
                in_=bank[:].rearrange("p t n -> p n t"),
            )

        def quantize_z(g, cols):
            if cols.start == 0:
                z_mx[g] = (kept("z%d_codes" % g, [PART, B], U32), kept("z%d_scales" % g, [PART, B], U8))
            codes, scales = z_mx[g]
            values = z_grouped[g][:, SLOTS * cols.start : SLOTS * cols.stop]
            nc.vector.quantize_mx(out=codes[:, cols].bitcast(FP8X4), scales=scales[:, cols], in_=values)

        def admittance(first, count, cols):
            width = cols.stop - cols.start
            bank = next_bank([PART, count, width])
            for n in range(count):
                half, tile_in_half = divmod(first + n, A_TILES // A_HALVES)
                rows = slice(tile_in_half * PART, (tile_in_half + 1) * PART)
                for g in range(H_PASSES):
                    nc.tensor.matmul_mx(
                        out=bank[:, n, :],
                        lhsT=v_mx[g, half][0][:, rows].bitcast(FP8X4),
                        lhsT_scale=v_mx[g, half][1][:, rows],
                        rhs=z_mx[g][0][:, cols].bitcast(FP8X4),
                        rhs_scale=z_mx[g][1][:, cols],
                        start=(g == 0),
                        stop=(g == H_PASSES - 1),
                    )
            result = staged("result", [PART, count, width], F32, 6)
            nc.vector.tensor_tensor(out=result[:], in0=bank[:], in1=y_ext_sb[:, first : first + count, cols], op=ADD)
            rows_out = out[first * PART : (first + count) * PART, cols]
            nc.sync.dma_start(out=rows_out.rearrange("(n p) b -> p n b", p=PART), in_=result[:])

        left, right, whole = slice(0, B // 2), slice(B // 2, B), slice(0, B)
        sort_modes("c_first", c_first, c_first_scales, [0])
        spread_y_mode()
        overlap_test(0, 0)
        group_trial(0)
        sort_modes("c_rest", c_rest, c_rest_scales, [1, 2])
        overlap_test(1, 0)
        group_trial(1)
        sort_fine(0, 0)
        quantize_trial(0)
        overlap_test(2, 0, range(0, 2))
        group_trial(2)
        turn_fine(0, 0)
        overlap_test(2, 0, range(2, 4))
        sort_fine(0, 1)
        quantize_trial(1)
        quantize_trial(2)
        turn_fine(0, 1)
        overlap_test(0, 1)
        sort_fine(1, 0)
        quantize_fine(0)
        turn_fine(1, 0)
        sort_fine(1, 1)
        group_v(0, 0)
        overlap_trial(0, 0)
        sort_fine(2, 0)
        turn_fine(1, 1)
        quantize_v(0, 0)
        overlap_trial(0, 1)
        group_v(1, 0)
        overlap_trial(0, 2)
        quantize_fine(1)
        overlap_trial(0, 3)
        quantize_v(1, 0)
        turn_fine(2, 0)
        sort_fine(2, 1)
        group_v(2, 0)
        overlap_test(1, 1)
        quantize_z(0, whole)
        overlap_trial(1, 0)
        quantize_v(2, 0)
        turn_fine(2, 1)
        overlap_trial(1, 1)
        group_v(0, 1)
        overlap_trial(1, 2)
        quantize_fine(2)
        overlap_trial(1, 3)
        quantize_v(0, 1)
        overlap_test(2, 1)
        group_v(1, 1)
        overlap_trial(2, 0)
        quantize_z(1, whole)
        overlap_trial(2, 1)
        quantize_v(1, 1)
        quantize_z(2, left)
        overlap_trial(2, 2)
        group_v(2, 1)
        overlap_trial(2, 3)
        quantize_z(2, right)
        admittance(0, 2, left)
        quantize_v(2, 1)
        admittance(2, 2, left)
        admittance(0, 2, right)
        admittance(2, 2, right)
        admittance(4, 2, left)
        admittance(6, 2, left)
        admittance(4, 2, right)
        admittance(6, 1, right)
        admittance(7, 1, right)
